import numpy as np
import ml_dtypes


def mxq(x, axis, fmt="e4m3"):
    dtype, down = {"e4m3": (ml_dtypes.float8_e4m3fn, 7), "e5m2": (ml_dtypes.float8_e5m2, 14)}[fmt]
    v = np.moveaxis(np.asarray(x, np.float32).astype(ml_dtypes.bfloat16).astype(np.float64), axis, -1)
    blocks = v.reshape(v.shape[:-1] + (-1, 32))
    amax = np.abs(blocks).max(-1, keepdims=True)
    byte = np.maximum(np.where(amax > 0, np.frexp(amax)[1] - 1 + 127, 0) - down, 1)
    scale = np.exp2(byte - 127.0)
    codes = (blocks / scale).astype(np.float32).astype(dtype).astype(np.float64)
    return np.moveaxis((codes * scale).reshape(v.shape), -1, axis)


WIDE = False


def mx_kscale(k):
    if not WIDE:
        return np.ones(k)
    levels = np.array([10, -10, 5, -5, 0])
    if k % 512:
        return np.exp2(np.random.permutation(np.resize(levels, k // 32))).repeat(32)
    a = np.empty((k // 512, 16))
    for p in range(k // 512):
        a[p, :8] = np.random.permutation(np.resize(levels, 8))
        for g in range(8):
            far = levels[np.abs(levels - a[p, g]) >= 10]
            a[p, g + 8] = far[np.random.randint(len(far))]
    return np.exp2(a.ravel()).repeat(32)


def f64(x):
    return np.asarray(x).astype(np.float64)


def striped(idx):
    return np.tile(idx.reshape(-1, 16).T, (8, 1)).astype(np.uint16)


def unstriped(offs):
    return offs[:16].T.reshape(-1).astype(np.int64)


E2M1 = np.array([0.0, 0.5, 1.0, 1.5, 2.0, 3.0, 4.0, 6.0, -0.0, -0.5, -1.0, -1.5, -2.0, -3.0, -4.0, -6.0])


def pack_weight(w, fmt):
    k, n = w.shape
    w = f64(np.asarray(w, np.float32).astype(ml_dtypes.bfloat16)).reshape(k // 32, 32, n)
    amax = np.abs(w).max(1)
    if fmt == "e4m3":
        byte = np.frexp(amax)[1] - 1 + 127 - 7
    else:
        mant, ex = np.frexp(amax / 6.0)
        byte = np.where(mant > 0.5, ex, ex - 1) + 127
    byte = np.clip(np.where(amax > 0, byte, 1), 1, 254)
    scaled = (w * np.exp2(127.0 - byte)[:, None, :]).reshape(k, n).astype(np.float32)
    by_word = np.ascontiguousarray(scaled.reshape(k // 512, 128, 4, n).transpose(0, 1, 3, 2))
    if fmt == "e4m3":
        words = by_word.astype(ml_dtypes.float8_e4m3fn).view(np.uint8)
    else:
        c = by_word.astype(ml_dtypes.float4_e2m1fn).view(np.uint8) & 0xF
        words = (c[..., 0::2] | (c[..., 1::2] << 4)).reshape(k // 512, 128, 2 * n)
    return np.ascontiguousarray(words), np.ascontiguousarray(byte.astype(np.uint8).reshape(k // 512, 16, n))


def unpack_weight(words, scales, fmt):
    g, _, n = scales.shape
    words = np.ascontiguousarray(words).reshape(g, 128, n, -1)
    if fmt == "e4m3":
        vals = words.view(ml_dtypes.float8_e4m3fn).astype(np.float64)
    else:
        nib = np.empty((g, 128, n, 4), np.uint8)
        nib[..., 0::2] = words & 0xF
        nib[..., 1::2] = words >> 4
        vals = E2M1[nib]
    vals = vals * np.repeat(np.exp2(scales.astype(np.float64) - 127.0), 8, axis=1)[..., None]
    return vals.transpose(0, 1, 3, 2).reshape(g * 512, n)


def gelu(v):
    return 0.5 * v * (1.0 + np.tanh(np.sqrt(2.0 / np.pi) * (v + 0.044715 * v**3)))


def bf(x):
    return np.asarray(x, np.float32).astype(ml_dtypes.bfloat16)


def planes(Y):
    n, m = Y.shape
    b = f64(bf(Y)).reshape(n // 32, 32, m)
    amax = np.abs(b).max(1)
    byte = np.clip(np.where(amax > 0, np.frexp(amax)[1] - 1 + 127 - 7, 1), 1, 254)
    codes = (b * np.exp2(127.0 - byte)[:, None, :]).reshape(n, m).astype(np.float32).astype(ml_dtypes.float8_e4m3fn).view(np.uint8)
    words = codes.reshape(n // 512, 128, 4, m).transpose(0, 1, 3, 2)
    return np.ascontiguousarray(words), np.ascontiguousarray(byte.astype(np.uint8).reshape(n // 512, 16, m))


K, T, S, K2, T2, P, H, N = 512, 4096, 1024, 1024, 2048, 512, 1024, 512

def setup_inputs():
    n = np.random.standard_normal
    s = mx_kscale(K)[:, None]
    s2 = mx_kscale(K2)[:, None]
    u = mx_kscale(H)[:, None]
    d = {}
    d["tab_words"], d["tab_scales"] = pack_weight(n((K, T)) * s, "e4m3")
    d["offs"] = striped(np.random.permutation(T)[:S])
    d["tab2_words"], d["tab2_scales"] = pack_weight(n((K2, T2)) * s2, "e4m3")
    d["offs2"] = striped(np.random.permutation(T2)[:P])
    d["pos1"] = striped(np.random.permutation(S)[:P])
    d["w1"] = (n((K, H)) / s * u.T / K ** 0.5).astype(np.float32)
    d["w2_words"], d["w2_scales"] = pack_weight(n((K, H)) / s / K ** 0.5, "e2m1")
    d["w3"] = (n((K, H)) / s * u.T / K ** 0.5).astype(np.float32)
    d["w4_words"], d["w4_scales"] = pack_weight(2.5 * n((K2, H)) / s2 / K2 ** 0.5, "e4m3")
    d["b4"] = n(H).astype(np.float32)
    d["gain"] = (2.5 * np.exp(0.3 * n(H)) * u[:, 0]).astype(np.float32)
    d["wgs"] = np.exp(0.3 * n((128, P))).astype(np.float32)
    d["w5"] = (0.5 * n((H, N)) / u * np.exp(0.8 * n(N)) / H ** 0.5).astype(np.float32)
    return d

def reference(tab_words, tab_scales, offs, tab2_words, tab2_scales, offs2, pos1, w1, w2_words, w2_scales,
              w3, w4_words, w4_scales, b4, gain, wgs, w5):
    v = unpack_weight(tab_words, tab_scales, "e4m3")[:, unstriped(offs)]
    v2 = unpack_weight(tab2_words, tab2_scales, "e4m3")[:, unstriped(offs2)]
    w2 = unpack_weight(w2_words, w2_scales, "e2m1")
    w4 = unpack_weight(w4_words, w4_scales, "e4m3")
    a1 = mxq(f64(w1), 0, "e4m3").T @ v
    a2 = w2.T @ v
    a3 = mxq(f64(w3), 0, "e4m3").T @ v
    a = a1 * a2 + a3
    b = f64(gain)[:, None] / (1.0 + np.exp(-((w4.T @ v2) + f64(b4)[:, None])))
    placed = np.zeros((H, S))
    placed[:, unstriped(pos1)] = np.tile(f64(wgs), (H // 128, 1)) * b
    z = a + placed
    y = mxq(f64(w5), 0, "e4m3").T @ mxq(z, 0, "e4m3")
    words, scales = planes(y)
    return y, words, scales

@@ -1,0 +1,453 @@
+from contextlib import ExitStack
+
+import concourse.mybir as mybir
+from concourse.masks import make_identity
+
+K, T, S, K2, T2, NP, H, N = 512, 4096, 1024, 1024, 2048, 512, 1024, 512
+FLOPS = 2 * (3 * K * H * S + K2 * H * NP + H * N * S)
+
+F32 = mybir.dt.float32
+BF16 = mybir.dt.bfloat16
+I32 = mybir.dt.int32
+U32 = mybir.dt.uint32
+U16 = mybir.dt.uint16
+U8 = mybir.dt.uint8
+E4M3 = mybir.dt.float8_e4m3fn_x4
+E2M1 = mybir.dt.float4_e2m1fn_x4
+MULT = mybir.AluOpType.mult
+ADD = mybir.AluOpType.add
+COPY = mybir.ActivationFunctionType.Copy
+SIGMOID = mybir.ActivationFunctionType.Sigmoid
+
+P = 128
+HALF = 512
+QUARTER = 256
+SLICES = H // P
+CHUNK = 256
+W4_FIRST = 128
+PAGES = 4
+RING = 4
+HELD = 4
+GATES = 2
+
+
+def tile_list_lesion_change_features_kernel(
+    tc, tab_words, tab_scales, offs, tab2_words, tab2_scales, offs2, pos1, w1, w2_words, w2_scales,
+    w3, w4_words, w4_scales, b4, gain, wgs, w5, out_0, out_1, out_2,
+):
+    nc = tc.nc
+    with ExitStack() as ctx:
+        lists = ctx.enter_context(tc.tile_pool(name="lists", bufs=1))
+        keep = ctx.enter_context(tc.tile_pool(name="keep", bufs=1))
+        psum = ctx.enter_context(tc.psum_pool(name="psum", bufs=1))
+
+        def sb(name, shape, dtype, after=None):
+            return keep.tile(shape, dtype, name=name, tag=after or name, align_bytes=64)
+
+        def ring(name, count, shape, dtype, after=None):
+            return [sb(name + str(i), shape, dtype, after and after + str(i)) for i in range(count)]
+
+        def words_of(dram):
+            return dram.rearrange("p n t -> p (n t)").bitcast(I32)
+
+        banks = [psum.tile([P, HALF], F32, name="bank" + str(i)) for i in range(8)]
+        a1_banks, scalar_banks, sum_banks, word_bank = banks[0:2], banks[2:5], banks[5:7], banks[7]
+
+        offs_sb = lists.tile([P, S // 16], U16, name="offs_sb")
+        offs2_sb = lists.tile([P, NP // 16], U16, name="offs2_sb")
+        pos1_sb = lists.tile([P, NP // 16], U16, name="pos1_sb")
+
+        t1_words = sb("t1_words", [P, T], I32)
+        t1_scales = sb("t1_scales", [P, T], U8)
+        t2_words = ring("t2_words", 2, [P, T2], I32)
+        t2_scales = sb("t2_scales", [P, T2], U8)
+        v1_words = ring("v1_words", 2, [P, HALF], U32)
+        v1_scales = ring("v1_scales", 2, [P, HALF], U8)
+        v2_words = ring("v2_words", 2, [P, NP], U32)
+        v2_scales = sb("v2_scales", [P, NP], U8)
+        w4_first = sb("w4_first", [P, 2, W4_FIRST], I32)
+        w4_rest = sb("w4_rest", [P, 2, H - W4_FIRST], I32)
+        w4_sc = sb("w4_sc", [P, H], U8)
+        w2_codes = sb("w2_codes", [P, 2 * H], U8)
+        w2_sc = sb("w2_sc", [P, H], U8)
+        w1_raw = ring("w1_raw", H // CHUNK, [P, 4, CHUNK], F32)
+        w3_raw = ring("w3_raw", H // CHUNK, [P, 4, CHUNK], F32)
+        w1_codes = ring("w1_codes", 2, [P, 512], U32)
+        w1_sc = ring("w1_sc", 2, [P, 512], U8)
+        w3_codes = ring("w3_codes", H // CHUNK, [P, CHUNK], U32)
+        w3_sc = ring("w3_sc", H // CHUNK, [P, CHUNK], U8)
+        w5_codes = ring("w5_codes", 2, [P, N], U32)
+        w5_sc = ring("w5_sc", 2, [P, N], U8)
+        w1_bf = ring("w1_bf", 2, [P, 4 * CHUNK], BF16)
+        w3_bf = ring("w3_bf", 2, [P, 4 * CHUNK], BF16)
+        w5_bf = ring("w5_bf", 2, [P, 4 * N], BF16)
+        rows = sb("rows", [P, P], F32)
+        columns = sb("columns", [P, 2 * SLICES], F32)
+        ident = sb("ident", [P, P], F32)
+        wgs_sb = sb("wgs_sb", [P, NP], F32)
+        factor = ring("factor", SLICES, [P, NP], F32)
+        gate = ring("gate", GATES, [P, NP], F32)
+        pages = ring("page", PAGES, [P, S], F32)
+        a2_sb = ring("a2_sb", RING, [P, HALF], F32)
+        a3_sb = ring("a3_sb", HELD, [P, HALF], F32)
+        a3_late = []
+        a2_late = ring("a2_late", 4, [P, HALF], F32)
+        prod = ring("prod", HELD, [P, HALF], F32)
+        zt = ring("zt", 2, [P, 4, 512], BF16)
+        z_bf = ring("z_bf", 4, [P, 4 * QUARTER], BF16)
+        z_codes = ring("z_codes", 8, [P, QUARTER], U32)
+        z_sc = ring("z_sc", 8, [P, QUARTER], U8)
+        y_bf = ring("y_bf", 2, [P, 4 * QUARTER], BF16)
+        y_codes = ring("y_codes", 4, [P, QUARTER], U32)
+        y_sc = sb("y_sc", [P, S], U8)
+
+        def load_scales(queue, tile, dram):
+            passes = dram.shape[0]
+            for q in range(4):
+                source = dram[:, 4 * q : 4 * q + 4, :] if passes > 1 else dram[0, 4 * q : 4 * q + 4, :]
+                queue.dma_start(out=tile[32 * q : 32 * q + 4 * passes, :].bitcast(I32), in_=source.bitcast(I32))
+
+        nc.gpsimd.memset(t2_scales[:].bitcast(I32), 0)
+        nc.gpsimd.memset(rows[:], 0.0)
+        nc.vector.memset(w4_sc[:].bitcast(I32), 0)
+        nc.vector.memset(t1_scales[:].bitcast(I32), 0)
+        nc.vector.memset(w2_sc[:].bitcast(I32), 0)
+        nc.vector.memset(pages[0][:], 0.0)
+
+        w4_view = w4_words.rearrange("a p n t -> p a (n t)").bitcast(I32)
+        w1_view = w1.rearrange("(p t) c -> p t c", t=4)
+        w3_view = w3.rearrange("(p t) c -> p t c", t=4)
+
+        def load_weights(c):
+            nc.sync.dma_start(out=w1_raw[c][:], in_=w1_view[:, :, c * CHUNK : (c + 1) * CHUNK])
+            nc.sync.dma_start(out=w3_raw[c][:], in_=w3_view[:, :, c * CHUNK : (c + 1) * CHUNK])
+
+        nc.sync.dma_start(offs2_sb[:], offs2)
+        nc.sync.dma_start(out=t2_words[0][:], in_=words_of(tab2_words[0]))
+        load_scales(nc.sync, t2_scales, tab2_scales)
+        nc.gpsimd.dma_start(out=rows[SLICES : 2 * SLICES, :], in_=gain.rearrange("(s p) -> s p", p=P))
+        nc.gpsimd.dma_start(out=rows[0:SLICES, :], in_=b4.rearrange("(s p) -> s p", p=P))
+        make_identity(nc, ident[:])
+        for page in pages[1:]:
+            nc.gpsimd.memset(page[:], 0.0)
+        nc.sync.dma_start(out=t2_words[1][:], in_=words_of(tab2_words[1]))
+        nc.sync.dma_start(out=wgs_sb[:], in_=wgs)
+        nc.sync.dma_start(out=w4_first[:], in_=w4_view[:, :, 0:W4_FIRST])
+        nc.sync.dma_start(pos1_sb[:], pos1)
+        load_scales(nc.sync, w4_sc, w4_scales)
+        nc.sync.dma_start(out=t1_words[:], in_=words_of(tab_words[0]))
+        nc.sync.dma_start(offs_sb[:], offs)
+        load_scales(nc.sync, t1_scales, tab_scales)
+        load_weights(0)
+        nc.sync.dma_start(out=w2_codes[:].bitcast(I32), in_=w2_words[0].bitcast(I32))
+        load_scales(nc.sync, w2_sc, w2_scales)
+        nc.sync.dma_start(out=w4_rest[:], in_=w4_view[:, :, W4_FIRST:H])
+        for c in range(1, H // CHUNK):
+            load_weights(c)
+
+        w5_raw = []
+
+        def gather_second():
+            nc.tensor.transpose(word_bank[:, 0:P], rows[:], ident[:])
+            nc.vector.tensor_copy(out=columns[:], in_=word_bank[:, 0 : 2 * SLICES])
+            nc.vector.tensor_copy(v2_words[0][:], t2_words[0][:].bitcast(U32).indirect(offs2_sb[:]))
+            nc.vector.tensor_copy(v2_scales[:], t2_scales[:].indirect(offs2_sb[:]))
+            nc.vector.tensor_copy(v2_words[1][:], t2_words[1][:].bitcast(U32).indirect(offs2_sb[:]))
+            w5_raw.extend(ring("w5_raw", 2, [P, 4, N], F32, after="t2_words"))
+            w5_view = w5.rearrange("(a p t) n -> a p t n", a=2, t=4)
+            for a in range(2):
+                nc.sync.dma_start(out=w5_raw[a][:], in_=w5_view[a])
+
+        turn = [0]
+
+        def scalar_bank():
+            turn[0] = turn[0] + 1
+            return scalar_banks[turn[0] % 3]
+
+        def confocal(s):
+            bank = scalar_bank()
+            tile, c0 = (w4_first, s * P) if s * P < W4_FIRST else (w4_rest, s * P - W4_FIRST)
+            for a in range(2):
+                nc.tensor.matmul_mx(
+                    bank[:],
+                    lhsT=tile[:, a, c0 : c0 + P].bitcast(E4M3),
+                    lhsT_scale=w4_sc[4 * a : P, s * P : (s + 1) * P],
+                    rhs=v2_words[a][:].bitcast(E4M3),
+                    rhs_scale=v2_scales[4 * a : P, :],
+                    start=(a == 0),
+                    stop=(a == 1),
+                )
+            nc.scalar.activation(gate[s % GATES][:], bank[:], SIGMOID, bias=columns[:, s : s + 1])
+
+        def weigh(s):
+            nc.vector.tensor_scalar(factor[s][:], wgs_sb[:], columns[:, SLICES + s : SLICES + s + 1], None, MULT)
+
+        def place(s):
+            nc.vector.tensor_tensor(pages[s % PAGES][:].indirect(pos1_sb[:]), gate[s % GATES][:], factor[s][:], MULT)
+
+        def gather_first(h):
+            part = offs_sb[:, h * (HALF // 16) : (h + 1) * (HALF // 16)]
+            nc.vector.tensor_copy(v1_words[h][:], t1_words[:].bitcast(U32).indirect(part))
+            nc.vector.tensor_copy(v1_scales[h][:], t1_scales[:].indirect(part))
+
+        def weave(copy, woven, raw):
+            copy(out=woven[:].rearrange("p (c i t) -> p c t i", i=4, t=4), in_=raw[:].rearrange("p t (c i) -> p c t i", i=4))
+
+        def prepare_w1(c):
+            weave(nc.scalar.copy, w1_bf[c % 2], w1_raw[c])
+            cols = slice(c % 2 * CHUNK, (c % 2 + 1) * CHUNK)
+            nc.vector.quantize_mx(w1_codes[c // 2][:, cols].bitcast(E4M3), w1_sc[c // 2][:, cols], w1_bf[c % 2][:])
+
+        def prepare_w3(c):
+            weave(nc.scalar.copy, w3_bf[c % 2], w3_raw[c])
+            nc.vector.quantize_mx(w3_codes[c][:].bitcast(E4M3), w3_sc[c][:], w3_bf[c % 2][:])
+
+        def round_w5(a):
+            nc.vector.tensor_copy(
+                out=w5_bf[a][:].rearrange("p (u m t) -> p m t u", u=4, t=4),
+                in_=w5_raw[a][:].rearrange("p t (m u) -> p m t u", u=4),
+            )
+
+        def quantise_w5(a):
+            nc.vector.quantize_mx(w5_codes[a][:].bitcast(E4M3), w5_sc[a][:], w5_bf[a][:])
+
+        def product(bank, codes, scales, h):
+            nc.tensor.matmul_mx(
+                bank[:], lhsT=codes, lhsT_scale=scales, rhs=v1_words[h][:].bitcast(E4M3), rhs_scale=v1_scales[h][:],
+                start=True, stop=True,
+            )
+
+        def second(s, h, i):
+            bank = scalar_bank()
+            product(bank, w2_codes[:, 2 * s * P : 2 * (s + 1) * P].bitcast(E2M1), w2_sc[:, s * P : (s + 1) * P], h)
+            nc.scalar.copy(out=a2_sb[i % RING][:], in_=bank[:])
+
+        def third(s, h, keep_in):
+            c, c0 = divmod(s * P, CHUNK)
+            bank = scalar_bank()
+            product(bank, w3_codes[c][:, c0 : c0 + P].bitcast(E4M3), w3_sc[c][:, c0 : c0 + P], h)
+            nc.scalar.copy(out=keep_in[:], in_=bank[:])
+
+        def first(s, h, i):
+            c, c0 = divmod(s * P, 512)
+            product(a1_banks[i % 2], w1_codes[c][:, c0 : c0 + P].bitcast(E4M3), w1_sc[c][:, c0 : c0 + P], h)
+            nc.vector.tensor_tensor(prod[i % HELD][:], a1_banks[i % 2][:], a2_sb[i % RING][:], MULT)
+
+        def add_transposed(bank, blocks, start, stop):
+            for n, (g, term) in enumerate(blocks):
+                nc.tensor.matmul(
+                    bank[:, g * P : (g + 1) * P], lhsT=term, rhs=ident[:], start=(start and n == 0),
+                    stop=(stop and n == len(blocks) - 1), is_transpose=True,
+                )
+
+        def blocks_of(ap):
+            return [(b, ap[:, b * P : (b + 1) * P]) for b in range(4)]
+
+        def page_half(s, h):
+            return pages[s % PAGES][:, h * HALF : (h + 1) * HALF]
+
+        def open_sum(i):
+            add_transposed(sum_banks[i % 2], blocks_of(a3_sb[i % HELD]) + blocks_of(prod[i % HELD]), True, False)
+
+        def close_sum(s, h, i):
+            bank = sum_banks[i % 2]
+            add_transposed(bank, blocks_of(page_half(s, h)), False, True)
+            a, g = divmod(s, 4)
+            nc.scalar.copy(
+                out=zt[2 * a + h][:].rearrange("j b (u g p e) -> j b u g p e", u=2, g=4, e=2)[:, :, :, g],
+                in_=bank[:].rearrange("j (b p u e) -> j b u p e", b=4, u=2, e=2),
+            )
+
+        def add_up(s, h, i):
+            open_sum(i)
+            close_sum(s, h, i)
+
+        def sorted_rows(tile):
+            return tile[:].rearrange("j (p u e) -> j u p e", u=2, e=2)
+
+        def as_sorted(ap):
+            return ap.rearrange("j (u p e) -> j u p e", u=2, e=2)
+
+        def late_product(bank, b, codes, scales):
+            cols = slice(b * P, (b + 1) * P)
+            nc.tensor.matmul_mx(
+                bank[:], lhsT=v1_words[1][:, cols].bitcast(E4M3), lhsT_scale=v1_scales[1][:, cols], rhs=codes,
+                rhs_scale=scales, start=True, stop=True,
+            )
+
+        def late_second(b):
+            bank = scalar_bank()
+            late_product(bank, b, w2_codes[:, H : 2 * H].bitcast(E2M1), w2_sc[:, 512:H])
+            nc.scalar.copy(out=as_sorted(a2_late[b][:]), in_=sorted_rows(bank))
+
+        def late_first(b):
+            late_product(a1_banks[b % 2], b, w1_codes[1][:].bitcast(E4M3), w1_sc[1][:])
+            nc.vector.tensor_tensor(
+                as_sorted(a2_late[b][:]), sorted_rows(a1_banks[b % 2]), as_sorted(a2_late[b][:]), MULT
+            )
+
+        def open_late_sum(b, bank):
+            cols = slice(b * P, (b + 1) * P)
+            blocks = [(g, a3_late[g][:, cols]) for g in range(4)] + [(g, page_half(4 + g, 1)[:, cols]) for g in range(3)]
+            add_transposed(bank, blocks, True, False)
+
+        def close_late_sum(b, bank):
+            add_transposed(bank, [(3, page_half(7, 1)[:, b * P : (b + 1) * P])], False, True)
+
+        def late_round(b, bank):
+            nc.vector.tensor_tensor(as_sorted(zt[3][:, b, :]), sorted_rows(bank), as_sorted(a2_late[b][:]), ADD)
+
+        def turn_back(a, q, bank, copy):
+            h, half = divmod(q, 2)
+            words = zt[2 * a + h][:].rearrange("j b r -> j (b r)").bitcast(F32)
+            for b in range(2):
+                for u in range(2):
+                    w0 = (2 * half + b) * 256 + u * P
+                    nc.tensor.transpose(bank[:, (2 * b + u) * P : (2 * b + u + 1) * P], words[:, w0 : w0 + P], ident[:])
+            copy(
+                out=z_bf[q][:].bitcast(F32).rearrange("p (b j u) -> p b j u", b=2, u=2),
+                in_=bank[:].rearrange("p (b u j) -> p b j u", b=2, u=2),
+            )
+
+        def quantise_z(a, q):
+            nc.vector.quantize_mx(z_codes[4 * a + q][:].bitcast(E4M3), z_sc[4 * a + q][:], z_bf[q][:])
+
+        y_sb = []
+
+        def last_product(q, pair_banks, copies):
+            for pair in range(2):
+                bank = pair_banks[pair]
+                for e in range(2):
+                    u = 2 * pair + e
+                    for a in range(2):
+                        nc.tensor.matmul_mx(
+                            bank[:, e * QUARTER : (e + 1) * QUARTER],
+                            lhsT=w5_codes[a][:, u * P : (u + 1) * P].bitcast(E4M3),
+                            lhsT_scale=w5_sc[a][:, u * P : (u + 1) * P],
+                            rhs=z_codes[4 * a + q][:].bitcast(E4M3),
+                            rhs_scale=z_sc[4 * a + q][:],
+                            start=(a == 0),
+                            stop=(a == 1),
+                        )
+                copies[pair](out=y_sb[q][:, 2 * pair : 2 * pair + 2, :].rearrange("p e j -> p (e j)"), in_=bank[:])
+            nc.sync.dma_start(
+                out=out_0.rearrange("(p t) s -> p t s", t=4)[:, :, q * QUARTER : (q + 1) * QUARTER], in_=y_sb[q][:]
+            )
+
+        def planes(q):
+            cols = slice(q * QUARTER, (q + 1) * QUARTER)
+            weave(nc.vector.tensor_copy, y_bf[q % 2], y_sb[q])
+            nc.vector.quantize_mx(y_codes[q][:].bitcast(E4M3), y_sc[:, cols], y_bf[q % 2][:])
+            nc.sync.dma_start(out=words_of(out_1[0])[:, cols], in_=y_codes[q][:].bitcast(I32))
+
+        on_scalar, on_vector = nc.scalar.copy, nc.vector.tensor_copy
+
+        gather_second()
+        weigh(0)
+        confocal(0)
+        place(0)
+        for s in range(1, SLICES):
+            weigh(s)
+        gather_first(0)
+        prepare_w1(0)
+        prepare_w3(0)
+        gather_first(1)
+        for s in range(4):
+            second(s, 0, 2 * s)
+            second(s, 1, 2 * s + 1)
+            first(s, 0, 2 * s)
+            first(s, 1, 2 * s + 1)
+            confocal(s + 1)
+            place(s + 1)
+            if s >= 1:
+                add_up(s - 1, 0, 2 * s - 2)
+                add_up(s - 1, 1, 2 * s - 1)
+            third(s, 0, a3_sb[(2 * s) % HELD])
+            third(s, 1, a3_sb[(2 * s + 1) % HELD])
+            if s >= 2:
+                late_second(s - 2)
+            if s % 2 == 0:
+                prepare_w1(s // 2 + 1)
+            else:
+                prepare_w3(s // 2 + 1)
+        zt.extend(ring("zt_b", 2, [P, 4, 512], BF16, after="w3_raw"))
+        a3_late.extend(ring("a3_late", 4, [P, HALF], F32, after="factor"))
+        def turn_first(q):
+            turn_back(0, q, word_bank, on_scalar)
+            quantise_z(0, q)
+
+        prepare_w1(3)
+        second(4, 0, 8)
+        first(4, 0, 8)
+        confocal(5)
+        place(5)
+        second(5, 0, 9)
+        first(5, 0, 9)
+        add_up(3, 0, 6)
+        add_up(3, 1, 7)
+        prepare_w3(3)
+        third(4, 0, a3_sb[8 % HELD])
+        third(4, 1, a3_late[0])
+        third(5, 1, a3_late[1])
+        round_w5(0)
+        quantise_w5(0)
+
+        confocal(6)
+        place(6)
+        second(6, 0, 10)
+        first(6, 0, 10)
+        add_up(4, 0, 8)
+        third(5, 0, a3_sb[9 % HELD])
+        third(6, 1, a3_late[2])
+        turn_first(0)
+        third(7, 1, a3_late[3])
+        turn_first(1)
+        round_w5(1)
+        quantise_w5(1)
+
+        third(6, 0, a3_sb[10 % HELD])
+        second(7, 0, 11)
+        first(7, 0, 11)
+        add_up(5, 0, 9)
+        confocal(7)
+        place(7)
+        third(7, 0, a3_sb[11 % HELD])
+        late_second(2)
+        late_second(3)
+        add_up(6, 0, 10)
+        turn_first(2)
+        turn_first(3)
+        y_sb.extend(ring("y_sb", 4, [P, 4, QUARTER], F32, after="w1_raw"))
+        late_banks = scalar_banks + [sum_banks[0]]
+        open_sum(11)
+        for b in range(4):
+            open_late_sum(b, late_banks[b])
+        close_sum(7, 0, 11)
+        for b in range(4):
+            close_late_sum(b, late_banks[b])
+        late_first(0)
+        late_first(1)
+        turn_back(1, 0, word_bank, on_scalar)
+        turn_back(1, 1, sum_banks[1], on_scalar)
+        late_round(0, late_banks[0])
+        late_round(1, late_banks[1])
+        quantise_z(1, 0)
+        late_first(2)
+        late_first(3)
+        turn_back(1, 2, word_bank, on_scalar)
+        quantise_z(1, 1)
+        last_product(0, late_banks[0:2], [on_scalar, on_scalar])
+        late_round(2, late_banks[2])
+        late_round(3, late_banks[3])
+        quantise_z(1, 2)
+        turn_back(1, 3, sum_banks[1], on_scalar)
+        last_product(1, a1_banks, [on_scalar, on_scalar])
+        planes(0)
+        quantise_z(1, 3)
+        last_product(2, late_banks[2:4], [on_scalar, on_scalar])
+        planes(1)
+        last_product(3, late_banks[0:2], [on_scalar, on_scalar])
+        planes(2)
+        planes(3)
+        for q in range(4):
+            nc.sync.dma_start(out=out_2[0, 4 * q : 4 * q + 4, :].bitcast(I32), in_=y_sc[32 * q : 32 * q + 4, :].bitcast(I32))

@@ -51,7 +51,7 @@ def tile_list_lesion_change_features_kernel(
             return dram.rearrange("p n t -> p (n t)").bitcast(I32)
 
         banks = [psum.tile([P, HALF], F32, name="bank" + str(i)) for i in range(8)]
-        a1_banks, scalar_banks, sum_banks, word_bank = banks[0:2], banks[2:5], banks[5:7], banks[7]
+        a1_banks, scalar_banks, sum_banks, word_bank = [], banks[0:5], banks[5:7], banks[7]
 
         offs_sb = lists.tile([P, S // 16], U16, name="offs_sb")
         offs2_sb = lists.tile([P, NP // 16], U16, name="offs2_sb")
@@ -85,7 +85,7 @@ def tile_list_lesion_change_features_kernel(
         columns = sb("columns", [P, 2 * SLICES], F32)
         ident = sb("ident", [P, P], F32)
         wgs_sb = sb("wgs_sb", [P, NP], F32)
-        factor = ring("factor", SLICES, [P, NP], F32)
+        factor = ring("factor", 4, [P, NP], F32)
         gate = ring("gate", GATES, [P, NP], F32)
         pages = ring("page", PAGES, [P, S], F32)
         a2_sb = ring("a2_sb", RING, [P, HALF], F32)
@@ -162,7 +162,7 @@ def tile_list_lesion_change_features_kernel(
 
         def scalar_bank():
             turn[0] = turn[0] + 1
-            return scalar_banks[turn[0] % 3]
+            return scalar_banks[turn[0] % 5]
 
         def confocal(s):
             bank = scalar_bank()
@@ -180,7 +180,11 @@ def tile_list_lesion_change_features_kernel(
             nc.scalar.activation(gate[s % GATES][:], bank[:], SIGMOID, bias=columns[:, s : s + 1])
 
         def weigh(s):
-            nc.vector.tensor_scalar(factor[s][:], wgs_sb[:], columns[:, SLICES + s : SLICES + s + 1], None, MULT)
+            gains = columns[:, SLICES + s : SLICES + s + 1]
+            if s < 4:
+                nc.vector.tensor_scalar(factor[s][:], wgs_sb[:], gains, None, MULT)
+            else:
+                nc.scalar.activation(factor[s][:], wgs_sb[:], COPY, scale=gains)
 
         def place(s):
             nc.vector.tensor_tensor(pages[s % PAGES][:].indirect(pos1_sb[:]), gate[s % GATES][:], factor[s][:], MULT)
@@ -230,8 +234,9 @@ def tile_list_lesion_change_features_kernel(
 
         def first(s, h, i):
             c, c0 = divmod(s * P, 512)
-            product(a1_banks[i % 2], w1_codes[c][:, c0 : c0 + P].bitcast(E4M3), w1_sc[c][:, c0 : c0 + P], h)
-            nc.vector.tensor_tensor(prod[i % HELD][:], a1_banks[i % 2][:], a2_sb[i % RING][:], MULT)
+            bank = scalar_bank()
+            product(bank, w1_codes[c][:, c0 : c0 + P].bitcast(E4M3), w1_sc[c][:, c0 : c0 + P], h)
+            nc.vector.tensor_tensor(prod[i % HELD][:], bank[:], a2_sb[i % RING][:], MULT)
 
         def add_transposed(bank, blocks, start, stop):
             for n, (g, term) in enumerate(blocks):
@@ -313,6 +318,7 @@ def tile_list_lesion_change_features_kernel(
             nc.vector.quantize_mx(z_codes[4 * a + q][:].bitcast(E4M3), z_sc[4 * a + q][:], z_bf[q][:])
 
         y_sb = []
+        y_rows = out_0.rearrange("(p t) s -> p t s", t=4)
 
         def last_product(q, pair_banks, copies):
             for pair in range(2):
@@ -329,16 +335,19 @@ def tile_list_lesion_change_features_kernel(
                             start=(a == 0),
                             stop=(a == 1),
                         )
-                copies[pair](out=y_sb[q][:, 2 * pair : 2 * pair + 2, :].rearrange("p e j -> p (e j)"), in_=bank[:])
-            nc.sync.dma_start(
-                out=out_0.rearrange("(p t) s -> p t s", t=4)[:, :, q * QUARTER : (q + 1) * QUARTER], in_=y_sb[q][:]
-            )
+                slots = slice(2 * pair, 2 * pair + 2)
+                copies[pair](out=y_sb[q][:, slots, :].rearrange("p e j -> p (e j)"), in_=bank[:])
+                if q == 3:
+                    nc.sync.dma_start(out=y_rows[:, slots, q * QUARTER : (q + 1) * QUARTER], in_=y_sb[q][:, slots, :])
+            if q < 3:
+                nc.sync.dma_start(out=y_rows[:, :, q * QUARTER : (q + 1) * QUARTER], in_=y_sb[q][:])
 
         def planes(q):
             cols = slice(q * QUARTER, (q + 1) * QUARTER)
             weave(nc.vector.tensor_copy, y_bf[q % 2], y_sb[q])
             nc.vector.quantize_mx(y_codes[q][:].bitcast(E4M3), y_sc[:, cols], y_bf[q % 2][:])
-            nc.sync.dma_start(out=words_of(out_1[0])[:, cols], in_=y_codes[q][:].bitcast(I32))
+            queue = nc.scalar if q == 3 else nc.sync
+            queue.dma_start(out=words_of(out_1[0])[:, cols], in_=y_codes[q][:].bitcast(I32))
 
         on_scalar, on_vector = nc.scalar.copy, nc.vector.tensor_copy
 
@@ -346,6 +355,8 @@ def tile_list_lesion_change_features_kernel(
         weigh(0)
         confocal(0)
         place(0)
+        later_factors = sb("later_factors", [P, 4, NP], F32, after="w4_first")
+        factor.extend([later_factors[:, n, :] for n in range(4)])
         for s in range(1, SLICES):
             weigh(s)
         gather_first(0)
@@ -364,77 +375,68 @@ def tile_list_lesion_change_features_kernel(
                 add_up(s - 1, 1, 2 * s - 1)
             third(s, 0, a3_sb[(2 * s) % HELD])
             third(s, 1, a3_sb[(2 * s + 1) % HELD])
-            if s >= 2:
-                late_second(s - 2)
             if s % 2 == 0:
                 prepare_w1(s // 2 + 1)
             else:
                 prepare_w3(s // 2 + 1)
+            if s >= 2:
+                late_second(s - 2)
         zt.extend(ring("zt_b", 2, [P, 4, 512], BF16, after="w3_raw"))
         a3_late.extend(ring("a3_late", 4, [P, HALF], F32, after="factor"))
-        def turn_first(q):
-            turn_back(0, q, word_bank, on_scalar)
+        def turn_first(q, bank=word_bank):
+            turn_back(0, q, bank, on_scalar)
             quantise_z(0, q)
 
-        prepare_w1(3)
-        second(4, 0, 8)
-        first(4, 0, 8)
-        confocal(5)
-        place(5)
-        second(5, 0, 9)
-        first(5, 0, 9)
-        add_up(3, 0, 6)
-        add_up(3, 1, 7)
-        prepare_w3(3)
-        third(4, 0, a3_sb[8 % HELD])
-        third(4, 1, a3_late[0])
-        third(5, 1, a3_late[1])
-        round_w5(0)
-        quantise_w5(0)
-
-        confocal(6)
-        place(6)
-        second(6, 0, 10)
-        first(6, 0, 10)
-        add_up(4, 0, 8)
-        third(5, 0, a3_sb[9 % HELD])
-        third(6, 1, a3_late[2])
-        turn_first(0)
-        third(7, 1, a3_late[3])
-        turn_first(1)
-        round_w5(1)
-        quantise_w5(1)
-
-        third(6, 0, a3_sb[10 % HELD])
+        for s in range(4, 7):
+            i = 4 + s
+            second(s, 0, i)
+            first(s, 0, i)
+            confocal(s + 1)
+            place(s + 1)
+            if s == 4:
+                prepare_w1(3)
+                add_up(3, 0, 6)
+                add_up(3, 1, 7)
+                prepare_w3(3)
+            else:
+                add_up(s - 1, 0, i - 1)
+            third(s, 0, a3_sb[i % HELD])
+            third(s, 1, a3_late[s - 4])
+            if s >= 5:
+                turn_first(2 * (s - 5))
+                late_second(s - 3)
+                turn_first(2 * (s - 5) + 1)
+            if s < 6:
+                round_w5(s - 4)
+                quantise_w5(s - 4)
         second(7, 0, 11)
         first(7, 0, 11)
-        add_up(5, 0, 9)
-        confocal(7)
-        place(7)
+        third(7, 1, a3_late[3])
         third(7, 0, a3_sb[11 % HELD])
-        late_second(2)
-        late_second(3)
         add_up(6, 0, 10)
-        turn_first(2)
-        turn_first(3)
         y_sb.extend(ring("y_sb", 4, [P, 4, QUARTER], F32, after="w1_raw"))
-        late_banks = scalar_banks + [sum_banks[0]]
-        open_sum(11)
-        for b in range(4):
-            open_late_sum(b, late_banks[b])
-        close_sum(7, 0, 11)
-        for b in range(4):
-            close_late_sum(b, late_banks[b])
+        a1_banks.extend([scalar_bank(), scalar_bank()])
+        late_banks = [word_bank, scalar_bank(), scalar_bank(), sum_banks[0]]
+        spare_bank = scalar_bank()
         late_first(0)
+        open_late_sum(0, late_banks[0])
+        close_late_sum(0, late_banks[0])
         late_first(1)
-        turn_back(1, 0, word_bank, on_scalar)
-        turn_back(1, 1, sum_banks[1], on_scalar)
+        add_up(7, 0, 11)
+        open_late_sum(1, late_banks[1])
+        close_late_sum(1, late_banks[1])
         late_round(0, late_banks[0])
-        late_round(1, late_banks[1])
-        quantise_z(1, 0)
         late_first(2)
+        turn_back(1, 0, spare_bank, on_scalar)
+        open_late_sum(2, late_banks[2])
+        close_late_sum(2, late_banks[2])
+        late_round(1, late_banks[1])
         late_first(3)
-        turn_back(1, 2, word_bank, on_scalar)
+        turn_back(1, 1, sum_banks[1], on_scalar)
+        open_late_sum(3, late_banks[3])
+        close_late_sum(3, late_banks[3])
+        quantise_z(1, 0)
+        turn_back(1, 2, spare_bank, on_scalar)
         quantise_z(1, 1)
         last_product(0, late_banks[0:2], [on_scalar, on_scalar])
         late_round(2, late_banks[2])
@@ -450,4 +452,5 @@ def tile_list_lesion_change_features_kernel(
         planes(2)
         planes(3)
         for q in range(4):
-            nc.sync.dma_start(out=out_2[0, 4 * q : 4 * q + 4, :].bitcast(I32), in_=y_sc[32 * q : 32 * q + 4, :].bitcast(I32))
+            queue = nc.scalar if q % 2 else nc.sync
+            queue.dma_start(out=out_2[0, 4 * q : 4 * q + 4, :].bitcast(I32), in_=y_sc[32 * q : 32 * q + 4, :].bitcast(I32))

@@ -20,15 +20,19 @@ COPY = mybir.ActivationFunctionType.Copy
 SIGMOID = mybir.ActivationFunctionType.Sigmoid
 
 P = 128
+PASS = 512
 HALF = 512
 QUARTER = 256
 SLICES = H // P
+PER_PASS = PASS // P
 CHUNK = 256
-W4_FIRST = 128
+W4_CUTS = (0, P, 2 * P, H)
 PAGES = 4
-RING = 4
-HELD = 4
 GATES = 2
+SECONDS = 6
+HELD = 4
+RING = 5
+VECTOR_FACTORS = 4
 
 
 def tile_list_lesion_change_features_kernel(
@@ -44,14 +48,14 @@ def tile_list_lesion_change_features_kernel(
         def sb(name, shape, dtype, after=None):
             return keep.tile(shape, dtype, name=name, tag=after or name, align_bytes=64)
 
-        def ring(name, count, shape, dtype, after=None):
-            return [sb(name + str(i), shape, dtype, after and after + str(i)) for i in range(count)]
+        def several(name, count, shape, dtype, after=None):
+            return [sb(name + str(n), shape, dtype, after and after + str(n)) for n in range(count)]
 
         def words_of(dram):
             return dram.rearrange("p n t -> p (n t)").bitcast(I32)
 
-        banks = [psum.tile([P, HALF], F32, name="bank" + str(i)) for i in range(8)]
-        a1_banks, scalar_banks, sum_banks, word_bank = [], banks[0:5], banks[5:7], banks[7]
+        banks = [psum.tile([P, HALF], F32, name="bank" + str(n)) for n in range(8)]
+        ring_banks, sum_banks, word_bank = banks[0:RING], banks[RING : RING + 2], banks[RING + 2]
 
         offs_sb = lists.tile([P, S // 16], U16, name="offs_sb")
         offs2_sb = lists.tile([P, NP // 16], U16, name="offs2_sb")
@@ -59,53 +63,45 @@ def tile_list_lesion_change_features_kernel(
 
         t1_words = sb("t1_words", [P, T], I32)
         t1_scales = sb("t1_scales", [P, T], U8)
-        t2_words = ring("t2_words", 2, [P, T2], I32)
+        t2_words = several("t2_words", 2, [P, T2], I32)
         t2_scales = sb("t2_scales", [P, T2], U8)
-        v1_words = ring("v1_words", 2, [P, HALF], U32)
-        v1_scales = ring("v1_scales", 2, [P, HALF], U8)
-        v2_words = ring("v2_words", 2, [P, NP], U32)
+        v1_words = several("v1_words", 1, [P, HALF], U32)
+        v1_scales = several("v1_scales", 2, [P, HALF], U8)
+        v2_words = several("v2_words", 2, [P, NP], U32)
         v2_scales = sb("v2_scales", [P, NP], U8)
-        w4_first = sb("w4_first", [P, 2, W4_FIRST], I32)
-        w4_rest = sb("w4_rest", [P, 2, H - W4_FIRST], I32)
+        w4_parts = [sb("w4_part" + str(n), [P, 2, W4_CUTS[n + 1] - W4_CUTS[n]], I32) for n in range(3)]
         w4_sc = sb("w4_sc", [P, H], U8)
         w2_codes = sb("w2_codes", [P, 2 * H], U8)
         w2_sc = sb("w2_sc", [P, H], U8)
-        w1_raw = ring("w1_raw", H // CHUNK, [P, 4, CHUNK], F32)
-        w3_raw = ring("w3_raw", H // CHUNK, [P, 4, CHUNK], F32)
-        w1_codes = ring("w1_codes", 2, [P, 512], U32)
-        w1_sc = ring("w1_sc", 2, [P, 512], U8)
-        w3_codes = ring("w3_codes", H // CHUNK, [P, CHUNK], U32)
-        w3_sc = ring("w3_sc", H // CHUNK, [P, CHUNK], U8)
-        w5_codes = ring("w5_codes", 2, [P, N], U32)
-        w5_sc = ring("w5_sc", 2, [P, N], U8)
-        w1_bf = ring("w1_bf", 2, [P, 4 * CHUNK], BF16)
-        w3_bf = ring("w3_bf", 2, [P, 4 * CHUNK], BF16)
-        w5_bf = ring("w5_bf", 2, [P, 4 * N], BF16)
+        w1_raw = several("w1_raw", H // CHUNK, [P, 4, CHUNK], F32)
+        w3_raw = several("w3_raw", H // CHUNK, [P, 4, CHUNK], F32)
+        w1_codes = several("w1_codes", 2, [P, PASS], U32)
+        w1_sc = several("w1_sc", 2, [P, PASS], U8)
+        w3_codes = several("w3_codes", H // CHUNK, [P, CHUNK], U32)
+        w3_sc = several("w3_sc", H // CHUNK, [P, CHUNK], U8)
+        w5_codes = several("w5_codes", 2, [P, N], U32)
+        w5_sc = several("w5_sc", 2, [P, N], U8)
+        w1_woven = several("w1_woven", 2, [P, 4 * CHUNK], BF16)
+        w3_woven = several("w3_woven", 2, [P, 4 * CHUNK], BF16)
+        w5_woven = several("w5_woven", 2, [P, 4 * N], BF16)
         rows = sb("rows", [P, P], F32)
         columns = sb("columns", [P, 2 * SLICES], F32)
         ident = sb("ident", [P, P], F32)
         wgs_sb = sb("wgs_sb", [P, NP], F32)
-        factor = ring("factor", 4, [P, NP], F32)
-        gate = ring("gate", GATES, [P, NP], F32)
-        pages = ring("page", PAGES, [P, S], F32)
-        a2_sb = ring("a2_sb", RING, [P, HALF], F32)
-        a3_sb = ring("a3_sb", HELD, [P, HALF], F32)
-        a3_late = []
-        a2_late = ring("a2_late", 4, [P, HALF], F32)
-        prod = ring("prod", HELD, [P, HALF], F32)
-        zt = ring("zt", 2, [P, 4, 512], BF16)
-        z_bf = ring("z_bf", 4, [P, 4 * QUARTER], BF16)
-        z_codes = ring("z_codes", 8, [P, QUARTER], U32)
-        z_sc = ring("z_sc", 8, [P, QUARTER], U8)
-        y_bf = ring("y_bf", 2, [P, 4 * QUARTER], BF16)
-        y_codes = ring("y_codes", 4, [P, QUARTER], U32)
+        factor = several("factor", VECTOR_FACTORS, [P, NP], F32)
+        gate = several("gate", GATES, [P, NP], F32)
+        pages = several("page", PAGES, [P, S], F32)
+        a2_sb = several("a2_sb", SECONDS - 1, [P, HALF], F32)
+        a3_sb = several("a3_sb", HELD, [P, HALF], F32)
+        late_acc = several("late_acc", PER_PASS, [P, PASS], F32)
+        prod = several("prod", HELD, [P, HALF], F32)
+        z_sorted = several("z_sorted", 2, [P, 4, PASS], BF16)
+        z_woven = several("z_woven", 4, [P, 4 * QUARTER], BF16)
+        z_codes = several("z_codes", 8, [P, QUARTER], U32)
+        z_sc = several("z_sc", 8, [P, QUARTER], U8)
+        y_woven = several("y_woven", 2, [P, 4 * QUARTER], BF16)
+        y_codes = several("y_codes", 4, [P, QUARTER], U32)
         y_sc = sb("y_sc", [P, S], U8)
-
-        def load_scales(queue, tile, dram):
-            passes = dram.shape[0]
-            for q in range(4):
-                source = dram[:, 4 * q : 4 * q + 4, :] if passes > 1 else dram[0, 4 * q : 4 * q + 4, :]
-                queue.dma_start(out=tile[32 * q : 32 * q + 4 * passes, :].bitcast(I32), in_=source.bitcast(I32))
 
         nc.gpsimd.memset(t2_scales[:].bitcast(I32), 0)
         nc.gpsimd.memset(rows[:], 0.0)
@@ -114,63 +110,71 @@ def tile_list_lesion_change_features_kernel(
         nc.vector.memset(w2_sc[:].bitcast(I32), 0)
         nc.vector.memset(pages[0][:], 0.0)
 
-        w4_view = w4_words.rearrange("a p n t -> p a (n t)").bitcast(I32)
-        w1_view = w1.rearrange("(p t) c -> p t c", t=4)
-        w3_view = w3.rearrange("(p t) c -> p t c", t=4)
+        def load_scales(tile, dram):
+            passes = dram.shape[0]
+            for q in range(4):
+                source = dram[:, 4 * q : 4 * q + 4, :] if passes > 1 else dram[0, 4 * q : 4 * q + 4, :]
+                nc.sync.dma_start(out=tile[32 * q : 32 * q + 4 * passes, :].bitcast(I32), in_=source.bitcast(I32))
 
-        def load_weights(c):
-            nc.sync.dma_start(out=w1_raw[c][:], in_=w1_view[:, :, c * CHUNK : (c + 1) * CHUNK])
-            nc.sync.dma_start(out=w3_raw[c][:], in_=w3_view[:, :, c * CHUNK : (c + 1) * CHUNK])
+        def load_w4(n):
+            view = w4_words.rearrange("a p n t -> p a (n t)").bitcast(I32)
+            nc.sync.dma_start(out=w4_parts[n][:], in_=view[:, :, W4_CUTS[n] : W4_CUTS[n + 1]])
+
+        def load_chunks(c):
+            for raw, dram in ((w1_raw, w1), (w3_raw, w3)):
+                view = dram.rearrange("(p t) c -> p t c", t=4)
+                nc.sync.dma_start(out=raw[c][:], in_=view[:, :, c * CHUNK : (c + 1) * CHUNK])
 
         nc.sync.dma_start(offs2_sb[:], offs2)
         nc.sync.dma_start(out=t2_words[0][:], in_=words_of(tab2_words[0]))
-        load_scales(nc.sync, t2_scales, tab2_scales)
+        load_scales(t2_scales, tab2_scales)
         nc.gpsimd.dma_start(out=rows[SLICES : 2 * SLICES, :], in_=gain.rearrange("(s p) -> s p", p=P))
         nc.gpsimd.dma_start(out=rows[0:SLICES, :], in_=b4.rearrange("(s p) -> s p", p=P))
         make_identity(nc, ident[:])
         for page in pages[1:]:
             nc.gpsimd.memset(page[:], 0.0)
         nc.sync.dma_start(out=t2_words[1][:], in_=words_of(tab2_words[1]))
-        nc.sync.dma_start(out=wgs_sb[:], in_=wgs)
-        nc.sync.dma_start(out=w4_first[:], in_=w4_view[:, :, 0:W4_FIRST])
+        load_w4(0)
         nc.sync.dma_start(pos1_sb[:], pos1)
-        load_scales(nc.sync, w4_sc, w4_scales)
+        load_scales(w4_sc, w4_scales)
+        nc.sync.dma_start(out=wgs_sb[:], in_=wgs)
         nc.sync.dma_start(out=t1_words[:], in_=words_of(tab_words[0]))
         nc.sync.dma_start(offs_sb[:], offs)
-        load_scales(nc.sync, t1_scales, tab_scales)
-        load_weights(0)
+        load_scales(t1_scales, tab_scales)
+        load_chunks(0)
         nc.sync.dma_start(out=w2_codes[:].bitcast(I32), in_=w2_words[0].bitcast(I32))
-        load_scales(nc.sync, w2_sc, w2_scales)
-        nc.sync.dma_start(out=w4_rest[:], in_=w4_view[:, :, W4_FIRST:H])
-        for c in range(1, H // CHUNK):
-            load_weights(c)
+        load_scales(w2_sc, w2_scales)
+        load_w4(1)
+        load_chunks(1)
+        load_w4(2)
+        load_chunks(2)
 
-        w5_raw = []
+        nc.tensor.transpose(word_bank[:, 0:P], rows[:], ident[:])
+        nc.vector.tensor_copy(out=columns[:], in_=word_bank[:, 0 : 2 * SLICES])
+        nc.vector.tensor_copy(v2_words[0][:], t2_words[0][:].bitcast(U32).indirect(offs2_sb[:]))
+        nc.vector.tensor_copy(v2_scales[:], t2_scales[:].indirect(offs2_sb[:]))
+        nc.vector.tensor_copy(v2_words[1][:], t2_words[1][:].bitcast(U32).indirect(offs2_sb[:]))
 
-        def gather_second():
-            nc.tensor.transpose(word_bank[:, 0:P], rows[:], ident[:])
-            nc.vector.tensor_copy(out=columns[:], in_=word_bank[:, 0 : 2 * SLICES])
-            nc.vector.tensor_copy(v2_words[0][:], t2_words[0][:].bitcast(U32).indirect(offs2_sb[:]))
-            nc.vector.tensor_copy(v2_scales[:], t2_scales[:].indirect(offs2_sb[:]))
-            nc.vector.tensor_copy(v2_words[1][:], t2_words[1][:].bitcast(U32).indirect(offs2_sb[:]))
-            w5_raw.extend(ring("w5_raw", 2, [P, 4, N], F32, after="t2_words"))
-            w5_view = w5.rearrange("(a p t) n -> a p t n", a=2, t=4)
-            for a in range(2):
-                nc.sync.dma_start(out=w5_raw[a][:], in_=w5_view[a])
+        w5_raw = several("w5_raw", 2, [P, 4, N], F32, after="t2_words")
+        w5_view = w5.rearrange("(a p t) n -> a p t n", a=2, t=4)
+        nc.sync.dma_start(out=w5_raw[0][:], in_=w5_view[0])
+        load_chunks(3)
+        nc.sync.dma_start(out=w5_raw[1][:], in_=w5_view[1])
 
-        turn = [0]
+        taken = [0]
 
-        def scalar_bank():
-            turn[0] = turn[0] + 1
-            return scalar_banks[turn[0] % 5]
+        def next_bank():
+            taken[0] = taken[0] + 1
+            return ring_banks[taken[0] % RING]
 
         def confocal(s):
-            bank = scalar_bank()
-            tile, c0 = (w4_first, s * P) if s * P < W4_FIRST else (w4_rest, s * P - W4_FIRST)
+            bank = next_bank()
+            n = min(s, 2)
+            c0 = s * P - W4_CUTS[n]
             for a in range(2):
                 nc.tensor.matmul_mx(
                     bank[:],
-                    lhsT=tile[:, a, c0 : c0 + P].bitcast(E4M3),
+                    lhsT=w4_parts[n][:, a, c0 : c0 + P].bitcast(E4M3),
                     lhsT_scale=w4_sc[4 * a : P, s * P : (s + 1) * P],
                     rhs=v2_words[a][:].bitcast(E4M3),
                     rhs_scale=v2_scales[4 * a : P, :],
@@ -181,7 +185,7 @@ def tile_list_lesion_change_features_kernel(
 
         def weigh(s):
             gains = columns[:, SLICES + s : SLICES + s + 1]
-            if s < 4:
+            if s < VECTOR_FACTORS:
                 nc.vector.tensor_scalar(factor[s][:], wgs_sb[:], gains, None, MULT)
             else:
                 nc.scalar.activation(factor[s][:], wgs_sb[:], COPY, scale=gains)
@@ -195,83 +199,74 @@ def tile_list_lesion_change_features_kernel(
             nc.vector.tensor_copy(v1_scales[h][:], t1_scales[:].indirect(part))
 
         def weave(copy, woven, raw):
-            copy(out=woven[:].rearrange("p (c i t) -> p c t i", i=4, t=4), in_=raw[:].rearrange("p t (c i) -> p c t i", i=4))
-
-        def prepare_w1(c):
-            weave(nc.scalar.copy, w1_bf[c % 2], w1_raw[c])
-            cols = slice(c % 2 * CHUNK, (c % 2 + 1) * CHUNK)
-            nc.vector.quantize_mx(w1_codes[c // 2][:, cols].bitcast(E4M3), w1_sc[c // 2][:, cols], w1_bf[c % 2][:])
-
-        def prepare_w3(c):
-            weave(nc.scalar.copy, w3_bf[c % 2], w3_raw[c])
-            nc.vector.quantize_mx(w3_codes[c][:].bitcast(E4M3), w3_sc[c][:], w3_bf[c % 2][:])
-
-        def round_w5(a):
-            nc.vector.tensor_copy(
-                out=w5_bf[a][:].rearrange("p (u m t) -> p m t u", u=4, t=4),
-                in_=w5_raw[a][:].rearrange("p t (m u) -> p m t u", u=4),
+            copy(
+                out=woven[:].rearrange("p (c i t) -> p c t i", i=4, t=4),
+                in_=raw[:].rearrange("p t (c i) -> p c t i", i=4),
             )
 
-        def quantise_w5(a):
-            nc.vector.quantize_mx(w5_codes[a][:].bitcast(E4M3), w5_sc[a][:], w5_bf[a][:])
+        def prepare_w1(c):
+            weave(nc.scalar.copy, w1_woven[c % 2], w1_raw[c])
+            cols = slice(c % 2 * CHUNK, (c % 2 + 1) * CHUNK)
+            nc.vector.quantize_mx(w1_codes[c // 2][:, cols].bitcast(E4M3), w1_sc[c // 2][:, cols], w1_woven[c % 2][:])
 
-        def product(bank, codes, scales, h):
+        def prepare_w3(c):
+            weave(nc.scalar.copy, w3_woven[c % 2], w3_raw[c])
+            nc.vector.quantize_mx(w3_codes[c][:].bitcast(E4M3), w3_sc[c][:], w3_woven[c % 2][:])
+
+        def prepare_w5(a):
+            nc.vector.tensor_copy(
+                out=w5_woven[a][:].rearrange("p (u m t) -> p m t u", u=4, t=4),
+                in_=w5_raw[a][:].rearrange("p t (m u) -> p m t u", u=4),
+            )
+            nc.vector.quantize_mx(w5_codes[a][:].bitcast(E4M3), w5_sc[a][:], w5_woven[a][:])
+
+        def step_of(s, h):
+            return 2 * s + h if s < PER_PASS else PER_PASS + s
+
+        def product(codes, scales, h):
+            bank = next_bank()
             nc.tensor.matmul_mx(
                 bank[:], lhsT=codes, lhsT_scale=scales, rhs=v1_words[h][:].bitcast(E4M3), rhs_scale=v1_scales[h][:],
                 start=True, stop=True,
             )
+            return bank
 
-        def second(s, h, i):
-            bank = scalar_bank()
-            product(bank, w2_codes[:, 2 * s * P : 2 * (s + 1) * P].bitcast(E2M1), w2_sc[:, s * P : (s + 1) * P], h)
-            nc.scalar.copy(out=a2_sb[i % RING][:], in_=bank[:])
+        def second(s, h):
+            bank = product(w2_codes[:, 2 * s * P : 2 * (s + 1) * P].bitcast(E2M1), w2_sc[:, s * P : (s + 1) * P], h)
+            nc.scalar.copy(out=a2_sb[step_of(s, h) % SECONDS][:], in_=bank[:])
 
-        def third(s, h, keep_in):
+        def first(s, h):
+            a, c0 = divmod(s * P, PASS)
+            bank = product(w1_codes[a][:, c0 : c0 + P].bitcast(E4M3), w1_sc[a][:, c0 : c0 + P], h)
+            i = step_of(s, h)
+            nc.vector.tensor_tensor(prod[i % HELD][:], bank[:], a2_sb[i % SECONDS][:], MULT)
+
+        def third(s, h):
             c, c0 = divmod(s * P, CHUNK)
-            bank = scalar_bank()
-            product(bank, w3_codes[c][:, c0 : c0 + P].bitcast(E4M3), w3_sc[c][:, c0 : c0 + P], h)
-            nc.scalar.copy(out=keep_in[:], in_=bank[:])
+            bank = product(w3_codes[c][:, c0 : c0 + P].bitcast(E4M3), w3_sc[c][:, c0 : c0 + P], h)
+            late = s >= PER_PASS and h == 1
+            nc.scalar.copy(out=(late_a3[s - PER_PASS] if late else a3_sb[step_of(s, h) % HELD])[:], in_=bank[:])
 
-        def first(s, h, i):
-            c, c0 = divmod(s * P, 512)
-            bank = scalar_bank()
-            product(bank, w1_codes[c][:, c0 : c0 + P].bitcast(E4M3), w1_sc[c][:, c0 : c0 + P], h)
-            nc.vector.tensor_tensor(prod[i % HELD][:], bank[:], a2_sb[i % RING][:], MULT)
-
-        def add_transposed(bank, blocks, start, stop):
+        def add_transposed(bank, blocks):
             for n, (g, term) in enumerate(blocks):
                 nc.tensor.matmul(
-                    bank[:, g * P : (g + 1) * P], lhsT=term, rhs=ident[:], start=(start and n == 0),
-                    stop=(stop and n == len(blocks) - 1), is_transpose=True,
+                    bank[:, g * P : (g + 1) * P], lhsT=term, rhs=ident[:], start=(n == 0),
+                    stop=(n == len(blocks) - 1), is_transpose=True,
                 )
-
-        def blocks_of(ap):
-            return [(b, ap[:, b * P : (b + 1) * P]) for b in range(4)]
 
         def page_half(s, h):
             return pages[s % PAGES][:, h * HALF : (h + 1) * HALF]
 
-        def open_sum(i):
-            add_transposed(sum_banks[i % 2], blocks_of(a3_sb[i % HELD]) + blocks_of(prod[i % HELD]), True, False)
-
-        def close_sum(s, h, i):
+        def add_up(s, h):
+            i = step_of(s, h)
             bank = sum_banks[i % 2]
-            add_transposed(bank, blocks_of(page_half(s, h)), False, True)
-            a, g = divmod(s, 4)
+            terms = [a3_sb[i % HELD], prod[i % HELD], page_half(s, h)]
+            add_transposed(bank, [(b, term[:, b * P : (b + 1) * P]) for term in terms for b in range(4)])
+            a, g = divmod(s, PER_PASS)
             nc.scalar.copy(
-                out=zt[2 * a + h][:].rearrange("j b (u g p e) -> j b u g p e", u=2, g=4, e=2)[:, :, :, g],
+                out=z_sorted[2 * a + h][:].rearrange("j b (u g p e) -> j b u g p e", u=2, g=4, e=2)[:, :, :, g],
                 in_=bank[:].rearrange("j (b p u e) -> j b u p e", b=4, u=2, e=2),
             )
-
-        def add_up(s, h, i):
-            open_sum(i)
-            close_sum(s, h, i)
-
-        def sorted_rows(tile):
-            return tile[:].rearrange("j (p u e) -> j u p e", u=2, e=2)
-
-        def as_sorted(ap):
-            return ap.rearrange("j (u p e) -> j u p e", u=2, e=2)
 
         def late_product(bank, b, codes, scales):
             cols = slice(b * P, (b + 1) * P)
@@ -281,46 +276,47 @@ def tile_list_lesion_change_features_kernel(
             )
 
         def late_second(b):
-            bank = scalar_bank()
-            late_product(bank, b, w2_codes[:, H : 2 * H].bitcast(E2M1), w2_sc[:, 512:H])
-            nc.scalar.copy(out=as_sorted(a2_late[b][:]), in_=sorted_rows(bank))
+            bank = next_bank()
+            late_product(bank, b, w2_codes[:, 2 * PASS : 2 * H].bitcast(E2M1), w2_sc[:, PASS:H])
+            nc.scalar.copy(out=late_acc[b][:], in_=bank[:])
 
         def late_first(b):
-            late_product(a1_banks[b % 2], b, w1_codes[1][:].bitcast(E4M3), w1_sc[1][:])
-            nc.vector.tensor_tensor(
-                as_sorted(a2_late[b][:]), sorted_rows(a1_banks[b % 2]), as_sorted(a2_late[b][:]), MULT
-            )
+            bank = late_first_banks[b % 2]
+            late_product(bank, b, w1_codes[1][:].bitcast(E4M3), w1_sc[1][:])
+            nc.vector.tensor_tensor(late_acc[b][:], bank[:], late_acc[b][:], MULT)
 
-        def open_late_sum(b, bank):
+        def late_sum(b):
             cols = slice(b * P, (b + 1) * P)
-            blocks = [(g, a3_late[g][:, cols]) for g in range(4)] + [(g, page_half(4 + g, 1)[:, cols]) for g in range(3)]
-            add_transposed(bank, blocks, True, False)
+            terms = [(g, late_a3[g][:, cols]) for g in range(PER_PASS)]
+            terms = terms + [(g, page_half(PER_PASS + g, 1)[:, cols]) for g in range(PER_PASS)]
+            add_transposed(late_sum_banks[b], terms)
 
-        def close_late_sum(b, bank):
-            add_transposed(bank, [(3, page_half(7, 1)[:, b * P : (b + 1) * P])], False, True)
+        def late_round(b):
+            nc.vector.tensor_tensor(z_late[b // 2][:, b % 2, :], late_sum_banks[b][:], late_acc[b][:], ADD)
 
-        def late_round(b, bank):
-            nc.vector.tensor_tensor(as_sorted(zt[3][:, b, :]), sorted_rows(bank), as_sorted(a2_late[b][:]), ADD)
-
-        def turn_back(a, q, bank, copy):
-            h, half = divmod(q, 2)
-            words = zt[2 * a + h][:].rearrange("j b r -> j (b r)").bitcast(F32)
+        def turn_back(a, q, bank):
+            h, pair = divmod(q, 2)
+            late = a == 1 and h == 1
+            words = (z_late[pair] if late else z_sorted[2 * a + h])[:].rearrange("j b r -> j (b r)").bitcast(F32)
             for b in range(2):
                 for u in range(2):
-                    w0 = (2 * half + b) * 256 + u * P
-                    nc.tensor.transpose(bank[:, (2 * b + u) * P : (2 * b + u + 1) * P], words[:, w0 : w0 + P], ident[:])
-            copy(
-                out=z_bf[q][:].bitcast(F32).rearrange("p (b j u) -> p b j u", b=2, u=2),
+                    w0 = (2 * pair + b) * 2 * P + u * P
+                    source = words[:, 2 * P * b + u : 2 * P * (b + 1) : 2] if late else words[:, w0 : w0 + P]
+                    nc.tensor.transpose(bank[:, (2 * b + u) * P : (2 * b + u + 1) * P], source, ident[:])
+            nc.scalar.copy(
+                out=z_woven[q][:].bitcast(F32).rearrange("p (b j u) -> p b j u", b=2, u=2),
                 in_=bank[:].rearrange("p (b u j) -> p b j u", b=2, u=2),
             )
 
         def quantise_z(a, q):
-            nc.vector.quantize_mx(z_codes[4 * a + q][:].bitcast(E4M3), z_sc[4 * a + q][:], z_bf[q][:])
+            nc.vector.quantize_mx(z_codes[4 * a + q][:].bitcast(E4M3), z_sc[4 * a + q][:], z_woven[q][:])
 
-        y_sb = []
-        y_rows = out_0.rearrange("(p t) s -> p t s", t=4)
+        def finish_first_pass(q):
+            turn_back(0, q, word_bank)
+            quantise_z(0, q)
 
-        def last_product(q, pair_banks, copies):
+        def last_product(q, pair_banks):
+            y_rows = out_0.rearrange("(p t) s -> p t s", t=4)
             for pair in range(2):
                 bank = pair_banks[pair]
                 for e in range(2):
@@ -335,120 +331,113 @@ def tile_list_lesion_change_features_kernel(
                             start=(a == 0),
                             stop=(a == 1),
                         )
-                slots = slice(2 * pair, 2 * pair + 2)
-                copies[pair](out=y_sb[q][:, slots, :].rearrange("p e j -> p (e j)"), in_=bank[:])
-                if q == 3:
-                    nc.sync.dma_start(out=y_rows[:, slots, q * QUARTER : (q + 1) * QUARTER], in_=y_sb[q][:, slots, :])
-            if q < 3:
-                nc.sync.dma_start(out=y_rows[:, :, q * QUARTER : (q + 1) * QUARTER], in_=y_sb[q][:])
+                both = slice(2 * pair, 2 * pair + 2)
+                nc.scalar.copy(out=y_sb[:, q, both, :].rearrange("p e j -> p (e j)"), in_=bank[:])
+                nc.sync.dma_start(out=y_rows[:, both, q * QUARTER : (q + 1) * QUARTER], in_=y_sb[:, q, both, :])
 
         def planes(q):
             cols = slice(q * QUARTER, (q + 1) * QUARTER)
-            weave(nc.vector.tensor_copy, y_bf[q % 2], y_sb[q])
-            nc.vector.quantize_mx(y_codes[q][:].bitcast(E4M3), y_sc[:, cols], y_bf[q % 2][:])
+            weave(nc.vector.tensor_copy, y_woven[q % 2], y_sb[:, q])
+            nc.vector.quantize_mx(y_codes[q][:].bitcast(E4M3), y_sc[:, cols], y_woven[q % 2][:])
             queue = nc.scalar if q == 3 else nc.sync
             queue.dma_start(out=words_of(out_1[0])[:, cols], in_=y_codes[q][:].bitcast(I32))
 
-        on_scalar, on_vector = nc.scalar.copy, nc.vector.tensor_copy
-
-        gather_second()
         weigh(0)
         confocal(0)
         place(0)
-        later_factors = sb("later_factors", [P, 4, NP], F32, after="w4_first")
-        factor.extend([later_factors[:, n, :] for n in range(4)])
+        scalar_factors = sb("scalar_factors", [P, SLICES - VECTOR_FACTORS, NP], F32, after="w4_part0")
+        factor.extend([scalar_factors[:, n, :] for n in range(SLICES - VECTOR_FACTORS)])
         for s in range(1, SLICES):
             weigh(s)
         gather_first(0)
         prepare_w1(0)
         prepare_w3(0)
+        v1_words.append(sb("v1_words_second", [P, HALF], U32, after="w1_raw0"))
+        a2_sb.insert(0, sb("a2_sb_first", [P, HALF], F32, after="w3_raw0"))
         gather_first(1)
-        for s in range(4):
-            second(s, 0, 2 * s)
-            second(s, 1, 2 * s + 1)
-            first(s, 0, 2 * s)
-            first(s, 1, 2 * s + 1)
+
+        chunk_slices = CHUNK // P
+        for s in range(chunk_slices):
+            second(s, 0)
+        for s in range(PER_PASS):
+            if s >= chunk_slices:
+                second(s, 0)
+            second(s, 1)
+            first(s, 0)
+            first(s, 1)
             confocal(s + 1)
             place(s + 1)
             if s >= 1:
-                add_up(s - 1, 0, 2 * s - 2)
-                add_up(s - 1, 1, 2 * s - 1)
-            third(s, 0, a3_sb[(2 * s) % HELD])
-            third(s, 1, a3_sb[(2 * s + 1) % HELD])
+                add_up(s - 1, 0)
+                add_up(s - 1, 1)
+            third(s, 0)
+            third(s, 1)
             if s % 2 == 0:
                 prepare_w1(s // 2 + 1)
             else:
                 prepare_w3(s // 2 + 1)
-            if s >= 2:
-                late_second(s - 2)
-        zt.extend(ring("zt_b", 2, [P, 4, 512], BF16, after="w3_raw"))
-        a3_late.extend(ring("a3_late", 4, [P, HALF], F32, after="factor"))
-        def turn_first(q, bank=word_bank):
-            turn_back(0, q, bank, on_scalar)
-            quantise_z(0, q)
+            if s >= chunk_slices:
+                late_second(s - chunk_slices)
 
-        for s in range(4, 7):
-            i = 4 + s
-            second(s, 0, i)
-            first(s, 0, i)
+        z_sorted.append(sb("z_sorted_last", [P, 4, PASS], BF16, after="w3_raw1"))
+        z_late = [sb("z_late" + str(n), [P, 2, PASS], BF16, after="w3_raw" + str(2 + n)) for n in range(2)]
+        late_a3 = several("late_a3", PER_PASS, [P, HALF], F32, after="factor")
+        last = SLICES - 1
+        for s in range(PER_PASS, last):
+            n = s - PER_PASS
+            second(s, 0)
+            first(s, 0)
             confocal(s + 1)
             place(s + 1)
-            if s == 4:
+            if n == 0:
                 prepare_w1(3)
-                add_up(3, 0, 6)
-                add_up(3, 1, 7)
+                add_up(s - 1, 0)
+                add_up(s - 1, 1)
                 prepare_w3(3)
             else:
-                add_up(s - 1, 0, i - 1)
-            third(s, 0, a3_sb[i % HELD])
-            third(s, 1, a3_late[s - 4])
-            if s >= 5:
-                turn_first(2 * (s - 5))
-                late_second(s - 3)
-                turn_first(2 * (s - 5) + 1)
-            if s < 6:
-                round_w5(s - 4)
-                quantise_w5(s - 4)
-        second(7, 0, 11)
-        first(7, 0, 11)
-        third(7, 1, a3_late[3])
-        third(7, 0, a3_sb[11 % HELD])
-        add_up(6, 0, 10)
-        y_sb.extend(ring("y_sb", 4, [P, 4, QUARTER], F32, after="w1_raw"))
-        a1_banks.extend([scalar_bank(), scalar_bank()])
-        late_banks = [word_bank, scalar_bank(), scalar_bank(), sum_banks[0]]
-        spare_bank = scalar_bank()
+                add_up(s - 1, 0)
+            third(s, 0)
+            third(s, 1)
+            if n >= 1:
+                finish_first_pass(2 * n - 2)
+                late_second(n + 1)
+                finish_first_pass(2 * n - 1)
+            if n < 2:
+                prepare_w5(n)
+        second(last, 0)
+        first(last, 0)
+        third(last, 1)
+        third(last, 0)
+        add_up(last - 1, 0)
+
+        y_sb = sb("y_sb", [P, 4, 4, QUARTER], F32, after="t1_words")
+        late_first_banks = [next_bank(), next_bank()]
+        late_sum_banks = [word_bank, next_bank(), next_bank(), sum_banks[0]]
+        turn_banks = [next_bank(), sum_banks[1]]
         late_first(0)
-        open_late_sum(0, late_banks[0])
-        close_late_sum(0, late_banks[0])
+        late_sum(0)
         late_first(1)
-        add_up(7, 0, 11)
-        open_late_sum(1, late_banks[1])
-        close_late_sum(1, late_banks[1])
-        late_round(0, late_banks[0])
-        late_first(2)
-        turn_back(1, 0, spare_bank, on_scalar)
-        open_late_sum(2, late_banks[2])
-        close_late_sum(2, late_banks[2])
-        late_round(1, late_banks[1])
-        late_first(3)
-        turn_back(1, 1, sum_banks[1], on_scalar)
-        open_late_sum(3, late_banks[3])
-        close_late_sum(3, late_banks[3])
+        add_up(last, 0)
+        for b in (1, 2):
+            late_sum(b)
+            late_round(b - 1)
+            late_first(b + 1)
+            turn_back(1, b - 1, turn_banks[b - 1])
+        late_sum(3)
         quantise_z(1, 0)
-        turn_back(1, 2, spare_bank, on_scalar)
+        turn_back(1, 2, turn_banks[0])
         quantise_z(1, 1)
-        last_product(0, late_banks[0:2], [on_scalar, on_scalar])
-        late_round(2, late_banks[2])
-        late_round(3, late_banks[3])
+        last_product(0, late_sum_banks[0:2])
+        late_round(2)
+        late_round(3)
         quantise_z(1, 2)
-        turn_back(1, 3, sum_banks[1], on_scalar)
-        last_product(1, a1_banks, [on_scalar, on_scalar])
+        turn_back(1, 3, turn_banks[1])
+        last_product(1, late_first_banks)
         planes(0)
         quantise_z(1, 3)
-        last_product(2, late_banks[2:4], [on_scalar, on_scalar])
+        last_product(2, late_sum_banks[2:4])
         planes(1)
-        last_product(3, late_banks[0:2], [on_scalar, on_scalar])
+        last_product(3, late_sum_banks[0:2])
         planes(2)
         planes(3)
         for q in range(4):

from contextlib import ExitStack

import concourse.mybir as mybir
from concourse.masks import make_identity

K, T, S, K2, T2, NP, H, N = 512, 4096, 1024, 1024, 2048, 512, 1024, 512
FLOPS = 2 * (3 * K * H * S + K2 * H * NP + H * N * S)

F32 = mybir.dt.float32
BF16 = mybir.dt.bfloat16
I32 = mybir.dt.int32
U32 = mybir.dt.uint32
U16 = mybir.dt.uint16
U8 = mybir.dt.uint8
E4M3 = mybir.dt.float8_e4m3fn_x4
E2M1 = mybir.dt.float4_e2m1fn_x4
MULT = mybir.AluOpType.mult
ADD = mybir.AluOpType.add
COPY = mybir.ActivationFunctionType.Copy
SIGMOID = mybir.ActivationFunctionType.Sigmoid

P = 128
PASS = 512
HALF = 512
QUARTER = 256
SLICES = H // P
PER_PASS = PASS // P
CHUNK = 256
W4_CUTS = (0, P, 2 * P, H)
PAGES = 4
GATES = 2
SECONDS = 6
HELD = 4
RING = 5
VECTOR_FACTORS = 4


def tile_list_lesion_change_features_kernel(
    tc, tab_words, tab_scales, offs, tab2_words, tab2_scales, offs2, pos1, w1, w2_words, w2_scales,
    w3, w4_words, w4_scales, b4, gain, wgs, w5, out_0, out_1, out_2,
):
    nc = tc.nc
    with ExitStack() as ctx:
        lists = ctx.enter_context(tc.tile_pool(name="lists", bufs=1))
        keep = ctx.enter_context(tc.tile_pool(name="keep", bufs=1))
        psum = ctx.enter_context(tc.psum_pool(name="psum", bufs=1))

        def sb(name, shape, dtype, after=None):
            return keep.tile(shape, dtype, name=name, tag=after or name, align_bytes=64)

        def several(name, count, shape, dtype, after=None):
            return [sb(name + str(n), shape, dtype, after and after + str(n)) for n in range(count)]

        def words_of(dram):
            return dram.rearrange("p n t -> p (n t)").bitcast(I32)

        banks = [psum.tile([P, HALF], F32, name="bank" + str(n)) for n in range(8)]
        ring_banks, sum_banks, word_bank = banks[0:RING], banks[RING : RING + 2], banks[RING + 2]

        offs_sb = lists.tile([P, S // 16], U16, name="offs_sb")
        offs2_sb = lists.tile([P, NP // 16], U16, name="offs2_sb")
        pos1_sb = lists.tile([P, NP // 16], U16, name="pos1_sb")

        t1_words = sb("t1_words", [P, T], I32)
        t1_scales = sb("t1_scales", [P, T], U8)
        t2_words = several("t2_words", 2, [P, T2], I32)
        t2_scales = sb("t2_scales", [P, T2], U8)
        v1_words = several("v1_words", 1, [P, HALF], U32)
        v1_scales = several("v1_scales", 2, [P, HALF], U8)
        v2_words = several("v2_words", 2, [P, NP], U32)
        v2_scales = sb("v2_scales", [P, NP], U8)
        w4_parts = [sb("w4_part" + str(n), [P, 2, W4_CUTS[n + 1] - W4_CUTS[n]], I32) for n in range(3)]
        w4_sc = sb("w4_sc", [P, H], U8)
        w2_codes = sb("w2_codes", [P, 2 * H], U8)
        w2_sc = sb("w2_sc", [P, H], U8)
        w1_raw = several("w1_raw", H // CHUNK, [P, 4, CHUNK], F32)
        w3_raw = several("w3_raw", H // CHUNK, [P, 4, CHUNK], F32)
        w1_codes = several("w1_codes", 2, [P, PASS], U32)
        w1_sc = several("w1_sc", 2, [P, PASS], U8)
        w3_codes = several("w3_codes", H // CHUNK, [P, CHUNK], U32)
        w3_sc = several("w3_sc", H // CHUNK, [P, CHUNK], U8)
        w5_codes = several("w5_codes", 2, [P, N], U32)
        w5_sc = several("w5_sc", 2, [P, N], U8)
        w1_woven = several("w1_woven", 2, [P, 4 * CHUNK], BF16)
        w3_woven = several("w3_woven", 2, [P, 4 * CHUNK], BF16)
        w5_woven = several("w5_woven", 2, [P, 4 * N], BF16)
        rows = sb("rows", [P, P], F32)
        columns = sb("columns", [P, 2 * SLICES], F32)
        ident = sb("ident", [P, P], F32)
        wgs_sb = sb("wgs_sb", [P, NP], F32)
        factor = several("factor", VECTOR_FACTORS, [P, NP], F32)
        gate = several("gate", GATES, [P, NP], F32)
        pages = several("page", PAGES, [P, S], F32)
        a2_sb = several("a2_sb", SECONDS - 1, [P, HALF], F32)
        a3_sb = several("a3_sb", HELD, [P, HALF], F32)
        late_acc = several("late_acc", PER_PASS, [P, PASS], F32)
        prod = several("prod", HELD, [P, HALF], F32)
        z_sorted = several("z_sorted", 2, [P, 4, PASS], BF16)
        z_woven = several("z_woven", 4, [P, 4 * QUARTER], BF16)
        z_codes = several("z_codes", 8, [P, QUARTER], U32)
        z_sc = several("z_sc", 8, [P, QUARTER], U8)
        y_woven = several("y_woven", 2, [P, 4 * QUARTER], BF16)
        y_codes = several("y_codes", 4, [P, QUARTER], U32)
        y_sc = sb("y_sc", [P, S], U8)

        nc.gpsimd.memset(t2_scales[:].bitcast(I32), 0)
        nc.gpsimd.memset(rows[:], 0.0)
        nc.vector.memset(w4_sc[:].bitcast(I32), 0)
        nc.vector.memset(t1_scales[:].bitcast(I32), 0)
        nc.vector.memset(w2_sc[:].bitcast(I32), 0)
        nc.vector.memset(pages[0][:], 0.0)

        def load_scales(tile, dram):
            passes = dram.shape[0]
            for q in range(4):
                source = dram[:, 4 * q : 4 * q + 4, :] if passes > 1 else dram[0, 4 * q : 4 * q + 4, :]
                nc.sync.dma_start(out=tile[32 * q : 32 * q + 4 * passes, :].bitcast(I32), in_=source.bitcast(I32))

        def load_w4(n):
            view = w4_words.rearrange("a p n t -> p a (n t)").bitcast(I32)
            nc.sync.dma_start(out=w4_parts[n][:], in_=view[:, :, W4_CUTS[n] : W4_CUTS[n + 1]])

        def load_chunks(c):
            for raw, dram in ((w1_raw, w1), (w3_raw, w3)):
                view = dram.rearrange("(p t) c -> p t c", t=4)
                nc.sync.dma_start(out=raw[c][:], in_=view[:, :, c * CHUNK : (c + 1) * CHUNK])

        nc.sync.dma_start(offs2_sb[:], offs2)
        nc.sync.dma_start(out=t2_words[0][:], in_=words_of(tab2_words[0]))
        load_scales(t2_scales, tab2_scales)
        nc.gpsimd.dma_start(out=rows[SLICES : 2 * SLICES, :], in_=gain.rearrange("(s p) -> s p", p=P))
        nc.gpsimd.dma_start(out=rows[0:SLICES, :], in_=b4.rearrange("(s p) -> s p", p=P))
        make_identity(nc, ident[:])
        for page in pages[1:]:
            nc.gpsimd.memset(page[:], 0.0)
        nc.sync.dma_start(out=t2_words[1][:], in_=words_of(tab2_words[1]))
        load_w4(0)
        nc.sync.dma_start(pos1_sb[:], pos1)
        load_scales(w4_sc, w4_scales)
        nc.sync.dma_start(out=wgs_sb[:], in_=wgs)
        nc.sync.dma_start(out=t1_words[:], in_=words_of(tab_words[0]))
        nc.sync.dma_start(offs_sb[:], offs)
        load_scales(t1_scales, tab_scales)
        load_chunks(0)
        nc.sync.dma_start(out=w2_codes[:].bitcast(I32), in_=w2_words[0].bitcast(I32))
        load_scales(w2_sc, w2_scales)
        load_w4(1)
        load_chunks(1)
        load_w4(2)
        load_chunks(2)

        nc.tensor.transpose(word_bank[:, 0:P], rows[:], ident[:])
        nc.vector.tensor_copy(out=columns[:], in_=word_bank[:, 0 : 2 * SLICES])
        nc.vector.tensor_copy(v2_words[0][:], t2_words[0][:].bitcast(U32).indirect(offs2_sb[:]))
        nc.vector.tensor_copy(v2_scales[:], t2_scales[:].indirect(offs2_sb[:]))
        nc.vector.tensor_copy(v2_words[1][:], t2_words[1][:].bitcast(U32).indirect(offs2_sb[:]))

        w5_raw = several("w5_raw", 2, [P, 4, N], F32, after="t2_words")
        w5_view = w5.rearrange("(a p t) n -> a p t n", a=2, t=4)
        nc.sync.dma_start(out=w5_raw[0][:], in_=w5_view[0])
        load_chunks(3)
        nc.sync.dma_start(out=w5_raw[1][:], in_=w5_view[1])

        taken = [0]

        def next_bank():
            taken[0] = taken[0] + 1
            return ring_banks[taken[0] % RING]

        def confocal(s):
            bank = next_bank()
            n = min(s, 2)
            c0 = s * P - W4_CUTS[n]
            for a in range(2):
                nc.tensor.matmul_mx(
                    bank[:],
                    lhsT=w4_parts[n][:, a, c0 : c0 + P].bitcast(E4M3),
                    lhsT_scale=w4_sc[4 * a : P, s * P : (s + 1) * P],
                    rhs=v2_words[a][:].bitcast(E4M3),
                    rhs_scale=v2_scales[4 * a : P, :],
                    start=(a == 0),
                    stop=(a == 1),
                )
            nc.scalar.activation(gate[s % GATES][:], bank[:], SIGMOID, bias=columns[:, s : s + 1])

        def weigh(s):
            gains = columns[:, SLICES + s : SLICES + s + 1]
            if s < VECTOR_FACTORS:
                nc.vector.tensor_scalar(factor[s][:], wgs_sb[:], gains, None, MULT)
            else:
                nc.scalar.activation(factor[s][:], wgs_sb[:], COPY, scale=gains)

        def place(s):
            nc.vector.tensor_tensor(pages[s % PAGES][:].indirect(pos1_sb[:]), gate[s % GATES][:], factor[s][:], MULT)

        def gather_first(h):
            part = offs_sb[:, h * (HALF // 16) : (h + 1) * (HALF // 16)]
            nc.vector.tensor_copy(v1_words[h][:], t1_words[:].bitcast(U32).indirect(part))
            nc.vector.tensor_copy(v1_scales[h][:], t1_scales[:].indirect(part))

        def weave(copy, woven, raw):
            copy(
                out=woven[:].rearrange("p (c i t) -> p c t i", i=4, t=4),
                in_=raw[:].rearrange("p t (c i) -> p c t i", i=4),
            )

        def prepare_w1(c):
            weave(nc.scalar.copy, w1_woven[c % 2], w1_raw[c])
            cols = slice(c % 2 * CHUNK, (c % 2 + 1) * CHUNK)
            nc.vector.quantize_mx(w1_codes[c // 2][:, cols].bitcast(E4M3), w1_sc[c // 2][:, cols], w1_woven[c % 2][:])

        def prepare_w3(c):
            weave(nc.scalar.copy, w3_woven[c % 2], w3_raw[c])
            nc.vector.quantize_mx(w3_codes[c][:].bitcast(E4M3), w3_sc[c][:], w3_woven[c % 2][:])

        def prepare_w5(a):
            nc.vector.tensor_copy(
                out=w5_woven[a][:].rearrange("p (u m t) -> p m t u", u=4, t=4),
                in_=w5_raw[a][:].rearrange("p t (m u) -> p m t u", u=4),
            )
            nc.vector.quantize_mx(w5_codes[a][:].bitcast(E4M3), w5_sc[a][:], w5_woven[a][:])

        def step_of(s, h):
            return 2 * s + h if s < PER_PASS else PER_PASS + s

        def product(codes, scales, h):
            bank = next_bank()
            nc.tensor.matmul_mx(
                bank[:], lhsT=codes, lhsT_scale=scales, rhs=v1_words[h][:].bitcast(E4M3), rhs_scale=v1_scales[h][:],
                start=True, stop=True,
            )
            return bank

        def second(s, h):
            bank = product(w2_codes[:, 2 * s * P : 2 * (s + 1) * P].bitcast(E2M1), w2_sc[:, s * P : (s + 1) * P], h)
            nc.scalar.copy(out=a2_sb[step_of(s, h) % SECONDS][:], in_=bank[:])

        def first(s, h):
            a, c0 = divmod(s * P, PASS)
            bank = product(w1_codes[a][:, c0 : c0 + P].bitcast(E4M3), w1_sc[a][:, c0 : c0 + P], h)
            i = step_of(s, h)
            nc.vector.tensor_tensor(prod[i % HELD][:], bank[:], a2_sb[i % SECONDS][:], MULT)

        def third(s, h):
            c, c0 = divmod(s * P, CHUNK)
            bank = product(w3_codes[c][:, c0 : c0 + P].bitcast(E4M3), w3_sc[c][:, c0 : c0 + P], h)
            late = s >= PER_PASS and h == 1
            nc.scalar.copy(out=(late_a3[s - PER_PASS] if late else a3_sb[step_of(s, h) % HELD])[:], in_=bank[:])

        def add_transposed(bank, blocks):
            for n, (g, term) in enumerate(blocks):
                nc.tensor.matmul(
                    bank[:, g * P : (g + 1) * P], lhsT=term, rhs=ident[:], start=(n == 0),
                    stop=(n == len(blocks) - 1), is_transpose=True,
                )

        def page_half(s, h):
            return pages[s % PAGES][:, h * HALF : (h + 1) * HALF]

        def add_up(s, h):
            i = step_of(s, h)
            bank = sum_banks[i % 2]
            terms = [a3_sb[i % HELD], prod[i % HELD], page_half(s, h)]
            add_transposed(bank, [(b, term[:, b * P : (b + 1) * P]) for term in terms for b in range(4)])
            a, g = divmod(s, PER_PASS)
            nc.scalar.copy(
                out=z_sorted[2 * a + h][:].rearrange("j b (u g p e) -> j b u g p e", u=2, g=4, e=2)[:, :, :, g],
                in_=bank[:].rearrange("j (b p u e) -> j b u p e", b=4, u=2, e=2),
            )

        def late_product(bank, b, codes, scales):
            cols = slice(b * P, (b + 1) * P)
            nc.tensor.matmul_mx(
                bank[:], lhsT=v1_words[1][:, cols].bitcast(E4M3), lhsT_scale=v1_scales[1][:, cols], rhs=codes,
                rhs_scale=scales, start=True, stop=True,
            )

        def late_second(b):
            bank = next_bank()
            late_product(bank, b, w2_codes[:, 2 * PASS : 2 * H].bitcast(E2M1), w2_sc[:, PASS:H])
            nc.scalar.copy(out=late_acc[b][:], in_=bank[:])

        def late_first(b):
            bank = late_first_banks[b % 2]
            late_product(bank, b, w1_codes[1][:].bitcast(E4M3), w1_sc[1][:])
            nc.vector.tensor_tensor(late_acc[b][:], bank[:], late_acc[b][:], MULT)

        def late_sum(b):
            cols = slice(b * P, (b + 1) * P)
            terms = [(g, late_a3[g][:, cols]) for g in range(PER_PASS)]
            terms = terms + [(g, page_half(PER_PASS + g, 1)[:, cols]) for g in range(PER_PASS)]
            add_transposed(late_sum_banks[b], terms)

        def late_round(b):
            nc.vector.tensor_tensor(z_late[b // 2][:, b % 2, :], late_sum_banks[b][:], late_acc[b][:], ADD)

        def turn_back(a, q, bank):
            h, pair = divmod(q, 2)
            late = a == 1 and h == 1
            words = (z_late[pair] if late else z_sorted[2 * a + h])[:].rearrange("j b r -> j (b r)").bitcast(F32)
            for b in range(2):
                for u in range(2):
                    w0 = (2 * pair + b) * 2 * P + u * P
                    source = words[:, 2 * P * b + u : 2 * P * (b + 1) : 2] if late else words[:, w0 : w0 + P]
                    nc.tensor.transpose(bank[:, (2 * b + u) * P : (2 * b + u + 1) * P], source, ident[:])
            nc.scalar.copy(
                out=z_woven[q][:].bitcast(F32).rearrange("p (b j u) -> p b j u", b=2, u=2),
                in_=bank[:].rearrange("p (b u j) -> p b j u", b=2, u=2),
            )

        def quantise_z(a, q):
            nc.vector.quantize_mx(z_codes[4 * a + q][:].bitcast(E4M3), z_sc[4 * a + q][:], z_woven[q][:])

        def finish_first_pass(q):
            turn_back(0, q, word_bank)
            quantise_z(0, q)

        def last_product(q, pair_banks):
            y_rows = out_0.rearrange("(p t) s -> p t s", t=4)
            for pair in range(2):
                bank = pair_banks[pair]
                for e in range(2):
                    u = 2 * pair + e
                    for a in range(2):
                        nc.tensor.matmul_mx(
                            bank[:, e * QUARTER : (e + 1) * QUARTER],
                            lhsT=w5_codes[a][:, u * P : (u + 1) * P].bitcast(E4M3),
                            lhsT_scale=w5_sc[a][:, u * P : (u + 1) * P],
                            rhs=z_codes[4 * a + q][:].bitcast(E4M3),
                            rhs_scale=z_sc[4 * a + q][:],
                            start=(a == 0),
                            stop=(a == 1),
                        )
                both = slice(2 * pair, 2 * pair + 2)
                nc.scalar.copy(out=y_sb[:, q, both, :].rearrange("p e j -> p (e j)"), in_=bank[:])
                nc.sync.dma_start(out=y_rows[:, both, q * QUARTER : (q + 1) * QUARTER], in_=y_sb[:, q, both, :])

        def planes(q):
            cols = slice(q * QUARTER, (q + 1) * QUARTER)
            weave(nc.vector.tensor_copy, y_woven[q % 2], y_sb[:, q])
            nc.vector.quantize_mx(y_codes[q][:].bitcast(E4M3), y_sc[:, cols], y_woven[q % 2][:])
            queue = nc.scalar if q == 3 else nc.sync
            queue.dma_start(out=words_of(out_1[0])[:, cols], in_=y_codes[q][:].bitcast(I32))

        weigh(0)
        confocal(0)
        place(0)
        scalar_factors = sb("scalar_factors", [P, SLICES - VECTOR_FACTORS, NP], F32, after="w4_part0")
        factor.extend([scalar_factors[:, n, :] for n in range(SLICES - VECTOR_FACTORS)])
        for s in range(1, SLICES):
            weigh(s)
        gather_first(0)
        prepare_w1(0)
        prepare_w3(0)
        v1_words.append(sb("v1_words_second", [P, HALF], U32, after="w1_raw0"))
        a2_sb.insert(0, sb("a2_sb_first", [P, HALF], F32, after="w3_raw0"))
        gather_first(1)

        chunk_slices = CHUNK // P
        for s in range(chunk_slices):
            second(s, 0)
        for s in range(PER_PASS):
            if s >= chunk_slices:
                second(s, 0)
            second(s, 1)
            first(s, 0)
            first(s, 1)
            confocal(s + 1)
            place(s + 1)
            if s >= 1:
                add_up(s - 1, 0)
                add_up(s - 1, 1)
            third(s, 0)
            third(s, 1)
            if s % 2 == 0:
                prepare_w1(s // 2 + 1)
            else:
                prepare_w3(s // 2 + 1)
            if s >= chunk_slices:
                late_second(s - chunk_slices)

        z_sorted.append(sb("z_sorted_last", [P, 4, PASS], BF16, after="w3_raw1"))
        z_late = [sb("z_late" + str(n), [P, 2, PASS], BF16, after="w3_raw" + str(2 + n)) for n in range(2)]
        late_a3 = several("late_a3", PER_PASS, [P, HALF], F32, after="factor")
        last = SLICES - 1
        for s in range(PER_PASS, last):
            n = s - PER_PASS
            second(s, 0)
            first(s, 0)
            confocal(s + 1)
            place(s + 1)
            if n == 0:
                prepare_w1(3)
                add_up(s - 1, 0)
                add_up(s - 1, 1)
                prepare_w3(3)
            else:
                add_up(s - 1, 0)
            third(s, 0)
            third(s, 1)
            if n >= 1:
                finish_first_pass(2 * n - 2)
                late_second(n + 1)
                finish_first_pass(2 * n - 1)
            if n < 2:
                prepare_w5(n)
        second(last, 0)
        first(last, 0)
        third(last, 1)
        third(last, 0)
        add_up(last - 1, 0)

        y_sb = sb("y_sb", [P, 4, 4, QUARTER], F32, after="t1_words")
        late_first_banks = [next_bank(), next_bank()]
        late_sum_banks = [word_bank, next_bank(), next_bank(), sum_banks[0]]
        turn_banks = [next_bank(), sum_banks[1]]
        late_first(0)
        late_sum(0)
        late_first(1)
        add_up(last, 0)
        for b in (1, 2):
            late_sum(b)
            late_round(b - 1)
            late_first(b + 1)
            turn_back(1, b - 1, turn_banks[b - 1])
        late_sum(3)
        quantise_z(1, 0)
        turn_back(1, 2, turn_banks[0])
        quantise_z(1, 1)
        last_product(0, late_sum_banks[0:2])
        late_round(2)
        late_round(3)
        quantise_z(1, 2)
        turn_back(1, 3, turn_banks[1])
        last_product(1, late_first_banks)
        planes(0)
        quantise_z(1, 3)
        last_product(2, late_sum_banks[2:4])
        planes(1)
        last_product(3, late_sum_banks[0:2])
        planes(2)
        planes(3)
        for q in range(4):
            queue = nc.scalar if q % 2 else nc.sync
            queue.dma_start(out=out_2[0, 4 * q : 4 * q + 4, :].bitcast(I32), in_=y_sc[32 * q : 32 * q + 4, :].bitcast(I32))
